import numpy as np, ml_dtypes
CORES = [16,32,48,64,80]
N = 5
import mx_ref
NC, G = 256, 2
C = np.float32(0.0085)
BF = ml_dtypes.bfloat16
def cut(t, i, w=512):
    return t[:, w * i:w * i + w]
def tile(rs):
    return np.stack(rs, axis=2).reshape(128, -1).astype(BF)
def layer(w, X):
    out = []
    for i in range(G):
        for t in range(len(X)):
            p = mx_ref.matmul(mx_ref.quantize(cut(w, len(X) * i + t)), X[t])
            z = p if t == 0 else z + p
        out.append(z)
    return out
def act(Z):
    return [np.maximum(s * z, 0) * C for z in Z for s in (1, -1)]
def setup_inputs(rng):
    def f(*shape):
        return mx_ref.flush((rng.standard_normal(shape, dtype=np.float32) * np.exp2(rng.integers(-2, 3, shape[:-1] + (1,)))).astype(BF))
    return {"x": f(N, 128, 4 * NC), "w1": f(N, 128, G * N * 512), "w2": f(N, 128, 2 * 512)}
def setup_inputs_blocks(rng):
    d = setup_inputs(rng)
    for k in ("x", "w1", "w2"): d[k] = mx_ref.spread(d[k], rng, 4)
    return d
def setup_inputs_wide(rng):
    d = setup_inputs(rng)
    for k in ("x", "w1", "w2"): d[k] = mx_ref.flush((d[k].astype(np.float32) * np.exp2(rng.integers(-6, 7, (N, 1, 1))).astype(np.float32)).astype(BF))
    return d
def reference(x, w1, w2, own=None):
    X = [mx_ref.quantize(x[j]) for j in range(N)]
    h = np.stack([tile(act(layer(w1[r], X))) for r in range(N)])
    use = h if own is None else own["h"]
    H = [mx_ref.quantize(use[j]) for j in range(N)]
    y = np.zeros((N, 128, NC), np.float32)
    for r in range(N):
        y[r] = mx_ref.matmul(mx_ref.quantize(cut(w2[r], 0)), H[r]) + mx_ref.matmul(mx_ref.quantize(cut(w2[r], 1)), H[(r + 1) % N])
    return {"h": h, "y": y}

@@ -1,0 +1,123 @@
+import numpy as np
+from concourse.bass import DstId, RemoteDMATransfer
+from concourse.mybir import dt, AluOpType, ActivationFunctionType
+
+N = 5
+NC = 256
+C = float(np.float32(0.0085))
+W1_PIECES = [(0, 2048), (2048, 4096), (4096, 5120)]
+
+SCRATCH = {
+    "xb": ("sbuf", [128, 4 * NC], "bfloat16"),
+    "w1b": ("sbuf", [128, 2 * N * 512], "bfloat16"),
+    "w2b": ("sbuf", [128, 2 * 512], "bfloat16"),
+    "hb": ("sbuf", [128, 4 * NC], "bfloat16"),
+    "yb": ("sbuf", [128, NC], "float32"),
+    "xq": ("sbuf", [128, N * NC], "float8_e4m3fn_x4"),
+    "xs": ("sbuf", [128, N * NC], "uint8"),
+    "w1q": ("sbuf", [128, 2 * N * 128], "float8_e4m3fn_x4"),
+    "w1s": ("sbuf", [128, 2 * N * 128], "uint8"),
+    "w2q": ("sbuf", [128, 2 * 128], "float8_e4m3fn_x4"),
+    "w2s": ("sbuf", [128, 2 * 128], "uint8"),
+    "hq": ("sbuf", [128, 2 * NC], "float8_e4m3fn_x4"),
+    "hs": ("sbuf", [128, 2 * NC], "uint8"),
+    "z0": ("psum", [128, 512], "float32"),
+    "z1": ("psum", [128, 512], "float32"),
+    "yp": ("psum", [128, 512], "float32"),
+}
+SEMAPHORES = ["lx", "lw0", "lw1", "lw2", "lv", "qx", "qw", "qv", "qh", "xa0", "xa1", "xa2", "xa3", "xa4",
+              "xl", "zd0", "zd1", "hr", "ha", "hl", "yd", "yc", "sh", "sy"]
+
+
+def _bits(mask):
+    return bin(mask).count("1")
+
+
+def _write(g, topo, dsts, view, mask, remote_sem, local_sem):
+    if len(dsts) == 1:
+        rid, pid, _ = topo.addr(dsts[0])
+        g.remote_dma(out_ap=view(True), in_ap=view(False), remote_sem=remote_sem, local_sem=local_sem,
+                     pid=pid, routing_id=rid, dma_engine_mask=mask)
+    else:
+        ids = [DstId(rid=topo.addr(d)[0], pnc=topo.addr(d)[1]) for d in dsts]
+        g.remote_dma_fused([RemoteDMATransfer(dst_ids=ids, dma_engine_mask=mask, remote_sem=remote_sem,
+                                              srcs=[view(False)], dsts=[view(True) for _ in dsts])],
+                           local_sem=local_sem)
+    return _bits(mask)
+
+
+def rank_program(g, core, T, topo):
+    r = T.rank_of(core)
+    if r is None:
+        return
+    S = T.sem
+    v, s, t, q = g.vector, g.scalar, g.tensor, g.sync
+    own = slice(NC * r, NC * r + NC)
+    after = [T.cores[(r + k) % N] for k in range(1, N)]
+    before = [(r - k) % N for k in range(1, N)]
+
+    q.dma_start(T.xb[:], T.x[:]).then_inc(S.lx, 16)
+    for p, (a, b) in enumerate(W1_PIECES):
+        (s if p % 2 == 0 else q).dma_start(T.w1b[:, a:b], T.w1[:, a:b]).then_inc(S["lw%d" % p], 16)
+    q.wait_ge(S["xa%d" % before[2]], 16)
+    q.dma_start(T.w2b[:], T.w2[:]).then_inc(S.lv, 16)
+
+    v.wait_ge(S.lx, 16)
+    v.quantize_mx(T.xq[:, own], T.xs[:, own], T.xb[:]).then_inc(S.qx, 1)
+    for p, (a, b) in enumerate(W1_PIECES):
+        v.wait_ge(S["lw%d" % p], 16)
+        v.quantize_mx(T.w1q[:, a // 4:b // 4], T.w1s[:, a // 4:b // 4], T.w1b[:, a:b]).then_inc(S.qw, 1)
+
+    g.wait_ge(S.qx, 1)
+    mask = topo.mask(core, after[0])
+    sent = _write(g, topo, after, lambda far: T.xs[:, own], mask, S["xa%d" % r], S.xl)
+    for d in after:
+        sent += _write(g, topo, [d], lambda far: T.xq[:, own].bitcast(dt.uint8), mask, S["xa%d" % r], S.xl)
+
+    t.wait_ge(S.qx, 1)
+    t.wait_ge(S.qw, len(W1_PIECES))
+    for n, j in enumerate([r] + before):
+        if j != r:
+            t.wait_ge(S["xa%d" % j], 16)
+        for i, z in enumerate((T.z0, T.z1)):
+            k = N * i + j
+            mm = t.matmul_mx(z[:, 0:NC], T.w1q[:, 128 * k:128 * k + 128], T.w1s[:, 128 * k:128 * k + 128],
+                             T.xq[:, NC * j:NC * j + NC], T.xs[:, NC * j:NC * j + NC], n == 0, n == N - 1)
+            if n == N - 1:
+                mm.then_inc(S["zd%d" % i], 1)
+
+    v.wait_ge(S.zd0, 1)
+    v.tensor_scalar(T.hb[:, 0:4 * NC:4], T.z0[:, 0:NC], 0.0, C, AluOpType.max, AluOpType.mult).then_inc(S.hr, 1)
+    v.tensor_scalar(T.hb[:, 1:4 * NC:4], T.z0[:, 0:NC], -C, 0.0, AluOpType.mult, AluOpType.max).then_inc(S.hr, 1)
+    s.wait_ge(S.zd1, 1)
+    s.activation(T.hb[:, 2:4 * NC:4], T.z1[:, 0:NC], ActivationFunctionType.Relu, scale=C).then_inc(S.hr, 1)
+    s.activation(T.hb[:, 3:4 * NC:4], T.z1[:, 0:NC], ActivationFunctionType.Relu, scale=-C).then_inc(S.hr, 1)
+    v.wait_ge(S.hr, 4)
+    v.quantize_mx(T.hq[:, 0:NC], T.hs[:, 0:NC], T.hb[:]).then_inc(S.qh, 1)
+
+    g.wait_ge(S.qh, 1)
+    prev = T.cores[(r - 1) % N]
+    hmask = topo.mask(core, prev)
+    left = _write(g, topo, [prev], lambda far: T.hq[:, NC:2 * NC].bitcast(dt.uint8) if far
+                  else T.hq[:, 0:NC].bitcast(dt.uint8), hmask, S.ha, S.hl)
+    left += _write(g, topo, [prev], lambda far: T.hs[:, NC:2 * NC] if far else T.hs[:, 0:NC], hmask, S.ha, S.hl)
+    s.wait_ge(S.hr, 4)
+    s.wait_ge(S.hl, left)
+    s.dma_start(T.h[:], T.hb[:]).then_inc(S.sh, 16)
+
+    v.wait_ge(S.lv, 16)
+    v.quantize_mx(T.w2q[:], T.w2s[:], T.w2b[:]).then_inc(S.qv, 1)
+    t.wait_ge(S.qh, 1)
+    t.wait_ge(S.qv, 1)
+    t.matmul_mx(T.yp[:, 0:NC], T.w2q[:, 0:128], T.w2s[:, 0:128], T.hq[:, 0:NC], T.hs[:, 0:NC], True, False)
+    t.wait_ge(S.ha, 16)
+    t.matmul_mx(T.yp[:, 0:NC], T.w2q[:, 128:256], T.w2s[:, 128:256], T.hq[:, NC:2 * NC], T.hs[:, NC:2 * NC],
+                False, True).then_inc(S.yd, 1)
+    v.wait_ge(S.yd, 1)
+    v.tensor_copy(T.yb[:], T.yp[:, 0:NC]).then_inc(S.yc, 1)
+    q.wait_ge(S.yc, 1)
+    q.dma_start(T.y[:], T.yb[:]).then_inc(S.sy, 16)
+
+    g.wait_ge(S.xl, sent)
+    s.wait_ge(S.sh, 16)
+    q.wait_ge(S.sy, 16)

@@ -4,6 +4,7 @@ from concourse.mybir import dt, AluOpType, ActivationFunctionType
 
 N = 5
 NC = 256
+HF = NC // 2
 C = float(np.float32(0.0085))
 W1_PIECES = [(0, 2048), (2048, 4096), (4096, 5120)]
 
@@ -12,7 +13,7 @@ SCRATCH = {
     "w1b": ("sbuf", [128, 2 * N * 512], "bfloat16"),
     "w2b": ("sbuf", [128, 2 * 512], "bfloat16"),
     "hb": ("sbuf", [128, 4 * NC], "bfloat16"),
-    "yb": ("sbuf", [128, NC], "float32"),
+    "yo": ("sbuf", [128, NC], "float32"),
     "xq": ("sbuf", [128, N * NC], "float8_e4m3fn_x4"),
     "xs": ("sbuf", [128, N * NC], "uint8"),
     "w1q": ("sbuf", [128, 2 * N * 128], "float8_e4m3fn_x4"),
@@ -21,45 +22,80 @@ SCRATCH = {
     "w2s": ("sbuf", [128, 2 * 128], "uint8"),
     "hq": ("sbuf", [128, 2 * NC], "float8_e4m3fn_x4"),
     "hs": ("sbuf", [128, 2 * NC], "uint8"),
-    "z0": ("psum", [128, 512], "float32"),
-    "z1": ("psum", [128, 512], "float32"),
-    "yp": ("psum", [128, 512], "float32"),
+    "z0a": ("psum", [128, 512], "float32"),
+    "z1a": ("psum", [128, 512], "float32"),
+    "z0b": ("psum", [128, 512], "float32"),
+    "z1b": ("psum", [128, 512], "float32"),
+    "ya": ("psum", [128, 512], "float32"),
+    "yb": ("psum", [128, 512], "float32"),
 }
-SEMAPHORES = ["lx", "lw0", "lw1", "lw2", "lv", "qx", "qw", "qv", "qh", "xa0", "xa1", "xa2", "xa3", "xa4",
-              "xl", "zd0", "zd1", "hr", "ha", "hl", "yd", "yc", "sh", "sy"]
+SEMAPHORES = ["lx", "lw0", "lw1", "lw2", "lv", "qx", "qw", "qv", "qh0", "qh1", "xa0", "xa1", "xa2", "xa3", "xa4",
+              "zb3", "zb4", "rc", "rs", "xl", "zd00", "zd01", "zd10", "zd11", "hr0", "hr1", "ha0", "ha1", "hl0", "hl1",
+              "yd0", "yd1", "yc0", "yc1", "sh0", "sh1", "sy0", "sy1"]
 
 
 def _bits(mask):
     return bin(mask).count("1")
 
 
-def _write(g, topo, dsts, view, mask, remote_sem, local_sem):
-    if len(dsts) == 1:
-        rid, pid, _ = topo.addr(dsts[0])
-        g.remote_dma(out_ap=view(True), in_ap=view(False), remote_sem=remote_sem, local_sem=local_sem,
-                     pid=pid, routing_id=rid, dma_engine_mask=mask)
-    else:
-        ids = [DstId(rid=topo.addr(d)[0], pnc=topo.addr(d)[1]) for d in dsts]
-        g.remote_dma_fused([RemoteDMATransfer(dst_ids=ids, dma_engine_mask=mask, remote_sem=remote_sem,
-                                              srcs=[view(False)], dsts=[view(True) for _ in dsts])],
-                           local_sem=local_sem)
+def _part(topo, dsts, src, dst, mask, remote_sem):
+    return RemoteDMATransfer(dst_ids=[DstId(rid=topo.addr(d)[0], pnc=topo.addr(d)[1]) for d in dsts],
+                             dma_engine_mask=mask, remote_sem=remote_sem, srcs=[src()], dsts=[dst() for _ in dsts])
+
+
+def _one(g, topo, d, src, dst, mask, remote_sem, local_sem):
+    rid, pid, _ = topo.addr(d)
+    g.remote_dma(out_ap=dst(), in_ap=src(), remote_sem=remote_sem, local_sem=local_sem,
+                 pid=pid, routing_id=rid, dma_engine_mask=mask)
     return _bits(mask)
 
 
+def _helper(rank_core, topo):
+    return [c for c in range(topo.CORES_PER_CHIP * topo.CHIPS)
+            if topo.chip(c) == topo.chip(rank_core) and topo.die(c) != topo.die(rank_core)][0]
+
+
+def _masks(rank_core, T, topo):
+    far = topo.mask(rank_core, [c for c in T.cores if c != rank_core][0])
+    return far, topo.mask(rank_core, _helper(rank_core, topo)) & ~far
+
+
 def rank_program(g, core, T, topo):
+    S = T.sem
+
+    def codes(j, a=0, b=NC):
+        return lambda: T.xq[:, NC * j + a:NC * j + b].bitcast(dt.uint8)
+
+    def plane(j):
+        return lambda: T.xs[:, NC * j:NC * j + NC]
+
     r = T.rank_of(core)
     if r is None:
+        for j, rc in enumerate(T.cores):
+            if core == _helper(rc, topo):
+                n = _bits(_masks(rc, T, topo)[1])
+                d = T.cores[(j + 4) % N]
+                m = topo.mask(core, d)
+                arr = S["xa%d" % j]
+                g.wait_ge(S.rc, n)
+                sent = _one(g, topo, d, codes(j, 0, HF), codes(j, 0, HF), m, arr, S.xl)
+                g.wait_ge(S.rs, n)
+                sent += _one(g, topo, d, plane(j), plane(j), m, arr, S.xl)
+                sent += _one(g, topo, d, codes(j, HF, NC), codes(j, HF, NC), m, S.zb4, S.xl)
+                g.wait_ge(S.xl, sent)
         return
-    S = T.sem
+
     v, s, t, q = g.vector, g.scalar, g.tensor, g.sync
     own = slice(NC * r, NC * r + NC)
-    after = [T.cores[(r + k) % N] for k in range(1, N)]
-    before = [(r - k) % N for k in range(1, N)]
+    d1, d2, d3 = [T.cores[(r + k) % N] for k in (1, 2, 3)]
+    j1, j2, j3, j4 = [(r - k) % N for k in (1, 2, 3, 4)]
+    Z = ((T.z0a, T.z1a), (T.z0b, T.z1b))
+    Y = (T.ya, T.yb)
 
     q.dma_start(T.xb[:], T.x[:]).then_inc(S.lx, 16)
     for p, (a, b) in enumerate(W1_PIECES):
         (s if p % 2 == 0 else q).dma_start(T.w1b[:, a:b], T.w1[:, a:b]).then_inc(S["lw%d" % p], 16)
-    q.wait_ge(S["xa%d" % before[2]], 16)
+    q.wait_ge(S["xa%d" % j2], 16)
     q.dma_start(T.w2b[:], T.w2[:]).then_inc(S.lv, 16)
 
     v.wait_ge(S.lx, 16)
@@ -68,56 +104,90 @@ def rank_program(g, core, T, topo):
         v.wait_ge(S["lw%d" % p], 16)
         v.quantize_mx(T.w1q[:, a // 4:b // 4], T.w1s[:, a // 4:b // 4], T.w1b[:, a:b]).then_inc(S.qw, 1)
 
+    far, near = _masks(core, T, topo)
+    hp = _helper(core, topo)
+    arr = S["xa%d" % r]
     g.wait_ge(S.qx, 1)
-    mask = topo.mask(core, after[0])
-    sent = _write(g, topo, after, lambda far: T.xs[:, own], mask, S["xa%d" % r], S.xl)
-    for d in after:
-        sent += _write(g, topo, [d], lambda far: T.xq[:, own].bitcast(dt.uint8), mask, S["xa%d" % r], S.xl)
+    g.remote_dma_fused([_part(topo, [hp], codes(r), codes(r), near, S.rc),
+                        _part(topo, [d1], codes(r), codes(r), far, arr)], local_sem=S.xl)
+    g.remote_dma_fused([_part(topo, [hp], plane(r), plane(r), near, S.rs),
+                        _part(topo, [d1, d2, d3], plane(r), plane(r), far, arr)], local_sem=S.xl)
+    sent = 2 * (_bits(near) + _bits(far))
+    sent += _one(g, topo, d2, codes(r), codes(r), far, arr, S.xl)
+    sent += _one(g, topo, d3, codes(r, 0, HF), codes(r, 0, HF), far, arr, S.xl)
+    sent += _one(g, topo, d3, codes(r, HF, NC), codes(r, HF, NC), far, S.zb3, S.xl)
+
+    def products(j, hf, first, last):
+        c = NC * j + HF * hf
+        for i in range(2):
+            k = N * i + j
+            mm = t.matmul_mx(Z[hf][i][:, 0:HF], T.w1q[:, 128 * k:128 * k + 128], T.w1s[:, 128 * k:128 * k + 128],
+                             T.xq[:, c:c + HF], T.xs[:, c:c + HF], first, last)
+            if last:
+                mm.then_inc(S["zd%d%d" % (hf, i)], 1)
 
     t.wait_ge(S.qx, 1)
     t.wait_ge(S.qw, len(W1_PIECES))
-    for n, j in enumerate([r] + before):
-        if j != r:
-            t.wait_ge(S["xa%d" % j], 16)
-        for i, z in enumerate((T.z0, T.z1)):
-            k = N * i + j
-            mm = t.matmul_mx(z[:, 0:NC], T.w1q[:, 128 * k:128 * k + 128], T.w1s[:, 128 * k:128 * k + 128],
-                             T.xq[:, NC * j:NC * j + NC], T.xs[:, NC * j:NC * j + NC], n == 0, n == N - 1)
-            if n == N - 1:
-                mm.then_inc(S["zd%d" % i], 1)
+    products(r, 0, True, False)
+    products(r, 1, True, False)
+    for j in (j1, j2):
+        t.wait_ge(S["xa%d" % j], 16)
+        products(j, 0, False, False)
+        products(j, 1, False, False)
+    t.wait_ge(S["xa%d" % j3], 16)
+    products(j3, 0, False, False)
+    t.wait_ge(S["xa%d" % j4], 16)
+    products(j4, 0, False, True)
+    t.wait_ge(S.zb3, 8)
+    products(j3, 1, False, False)
+    t.wait_ge(S.zb4, 8)
+    products(j4, 1, False, True)
 
-    v.wait_ge(S.zd0, 1)
-    v.tensor_scalar(T.hb[:, 0:4 * NC:4], T.z0[:, 0:NC], 0.0, C, AluOpType.max, AluOpType.mult).then_inc(S.hr, 1)
-    v.tensor_scalar(T.hb[:, 1:4 * NC:4], T.z0[:, 0:NC], -C, 0.0, AluOpType.mult, AluOpType.max).then_inc(S.hr, 1)
-    s.wait_ge(S.zd1, 1)
-    s.activation(T.hb[:, 2:4 * NC:4], T.z1[:, 0:NC], ActivationFunctionType.Relu, scale=C).then_inc(S.hr, 1)
-    s.activation(T.hb[:, 3:4 * NC:4], T.z1[:, 0:NC], ActivationFunctionType.Relu, scale=-C).then_inc(S.hr, 1)
-    v.wait_ge(S.hr, 4)
-    v.quantize_mx(T.hq[:, 0:NC], T.hs[:, 0:NC], T.hb[:]).then_inc(S.qh, 1)
-
-    g.wait_ge(S.qh, 1)
     prev = T.cores[(r - 1) % N]
     hmask = topo.mask(core, prev)
-    left = _write(g, topo, [prev], lambda far: T.hq[:, NC:2 * NC].bitcast(dt.uint8) if far
-                  else T.hq[:, 0:NC].bitcast(dt.uint8), hmask, S.ha, S.hl)
-    left += _write(g, topo, [prev], lambda far: T.hs[:, NC:2 * NC] if far else T.hs[:, 0:NC], hmask, S.ha, S.hl)
-    s.wait_ge(S.hr, 4)
-    s.wait_ge(S.hl, left)
-    s.dma_start(T.h[:], T.hb[:]).then_inc(S.sh, 16)
+    left = [0, 0]
+    for hf in range(2):
+        lo, hi = 4 * HF * hf, 4 * HF * (hf + 1)
+        a, b = HF * hf, HF * (hf + 1)
+        hr = S["hr%d" % hf]
+        v.wait_ge(S["zd%d0" % hf], 1)
+        v.tensor_scalar(T.hb[:, lo:hi:4], Z[hf][0][:, 0:HF], 0.0, C, AluOpType.max, AluOpType.mult).then_inc(hr, 1)
+        v.tensor_scalar(T.hb[:, lo + 1:hi:4], Z[hf][0][:, 0:HF], -C, 0.0, AluOpType.mult, AluOpType.max).then_inc(hr, 1)
+        s.wait_ge(S["zd%d1" % hf], 1)
+        s.activation(T.hb[:, lo + 2:hi:4], Z[hf][1][:, 0:HF], ActivationFunctionType.Relu, scale=C).then_inc(hr, 1)
+        s.activation(T.hb[:, lo + 3:hi:4], Z[hf][1][:, 0:HF], ActivationFunctionType.Relu, scale=-C).then_inc(hr, 1)
+        v.wait_ge(hr, 4)
+        v.quantize_mx(T.hq[:, a:b], T.hs[:, a:b], T.hb[:, lo:hi]).then_inc(S["qh%d" % hf], 1)
+        g.wait_ge(S["qh%d" % hf], 1)
+        left[hf] += _one(g, topo, prev, lambda: T.hq[:, a:b].bitcast(dt.uint8),
+                         lambda: T.hq[:, NC + a:NC + b].bitcast(dt.uint8), hmask, S["ha%d" % hf], S["hl%d" % hf])
+        left[hf] += _one(g, topo, prev, lambda: T.hs[:, a:b], lambda: T.hs[:, NC + a:NC + b], hmask,
+                         S["ha%d" % hf], S["hl%d" % hf])
+
+    for hf in range(2):
+        lo, hi = 4 * HF * hf, 4 * HF * (hf + 1)
+        s.wait_ge(S["hr%d" % hf], 4)
+        s.wait_ge(S["hl%d" % hf], left[hf])
+        s.dma_start(T.h[:, lo:hi], T.hb[:, lo:hi]).then_inc(S["sh%d" % hf], 16)
 
     v.wait_ge(S.lv, 16)
     v.quantize_mx(T.w2q[:], T.w2s[:], T.w2b[:]).then_inc(S.qv, 1)
-    t.wait_ge(S.qh, 1)
     t.wait_ge(S.qv, 1)
-    t.matmul_mx(T.yp[:, 0:NC], T.w2q[:, 0:128], T.w2s[:, 0:128], T.hq[:, 0:NC], T.hs[:, 0:NC], True, False)
-    t.wait_ge(S.ha, 16)
-    t.matmul_mx(T.yp[:, 0:NC], T.w2q[:, 128:256], T.w2s[:, 128:256], T.hq[:, NC:2 * NC], T.hs[:, NC:2 * NC],
-                False, True).then_inc(S.yd, 1)
-    v.wait_ge(S.yd, 1)
-    v.tensor_copy(T.yb[:], T.yp[:, 0:NC]).then_inc(S.yc, 1)
-    q.wait_ge(S.yc, 1)
-    q.dma_start(T.y[:], T.yb[:]).then_inc(S.sy, 16)
+    for hf in range(2):
+        a, b = HF * hf, HF * (hf + 1)
+        t.wait_ge(S["qh%d" % hf], 1)
+        t.matmul_mx(Y[hf][:, 0:HF], T.w2q[:, 0:128], T.w2s[:, 0:128], T.hq[:, a:b], T.hs[:, a:b], True, False)
+    for hf in range(2):
+        a, b = HF * hf, HF * (hf + 1)
+        t.wait_ge(S["ha%d" % hf], 16)
+        t.matmul_mx(Y[hf][:, 0:HF], T.w2q[:, 128:256], T.w2s[:, 128:256], T.hq[:, NC + a:NC + b],
+                    T.hs[:, NC + a:NC + b], False, True).then_inc(S["yd%d" % hf], 1)
+        v.wait_ge(S["yd%d" % hf], 1)
+        v.tensor_copy(T.yo[:, a:b], Y[hf][:, 0:HF]).then_inc(S["yc%d" % hf], 1)
+        q.wait_ge(S["yc%d" % hf], 1)
+        q.dma_start(T.y[:, a:b], T.yo[:, a:b]).then_inc(S["sy%d" % hf], 16)
 
     g.wait_ge(S.xl, sent)
-    s.wait_ge(S.sh, 16)
-    q.wait_ge(S.sy, 16)
+    for hf in range(2):
+        s.wait_ge(S["sh%d" % hf], 16)
+        q.wait_ge(S["sy%d" % hf], 16)

@@ -29,8 +29,9 @@ SCRATCH = {
     "ya": ("psum", [128, 512], "float32"),
     "yb": ("psum", [128, 512], "float32"),
 }
-SEMAPHORES = ["lx", "lw0", "lw1", "lw2", "lv", "qx", "qw", "qv", "qh0", "qh1", "xa0", "xa1", "xa2", "xa3", "xa4",
-              "zb3", "zb4", "rc", "rs", "xl", "zd00", "zd01", "zd10", "zd11", "hr0", "hr1", "ha0", "ha1", "hl0", "hl1",
+SEMAPHORES = ["lxa", "lxb", "lw0", "lw1", "lw2", "lv", "qxa", "qxb", "qw", "qv", "qh0", "qh1",
+              "xa0", "xa1", "xa2", "xa3", "xa4", "xb0", "xb1", "xb2", "xb3", "xb4",
+              "rca", "rcb", "rs", "xl", "zd00", "zd01", "zd10", "zd11", "hr0", "hr1", "ha0", "ha1", "hl0", "hl1",
               "yd0", "yd1", "yc0", "yc1", "sh0", "sh1", "sy0", "sy1"]
 
 
@@ -38,9 +39,9 @@ def _bits(mask):
     return bin(mask).count("1")
 
 
-def _part(topo, dsts, src, dst, mask, remote_sem):
+def _part(topo, dsts, ap, mask, remote_sem):
     return RemoteDMATransfer(dst_ids=[DstId(rid=topo.addr(d)[0], pnc=topo.addr(d)[1]) for d in dsts],
-                             dma_engine_mask=mask, remote_sem=remote_sem, srcs=[src()], dsts=[dst() for _ in dsts])
+                             dma_engine_mask=mask, remote_sem=remote_sem, srcs=[ap()], dsts=[ap() for _ in dsts])
 
 
 def _one(g, topo, d, src, dst, mask, remote_sem, local_sem):
@@ -50,21 +51,21 @@ def _one(g, topo, d, src, dst, mask, remote_sem, local_sem):
     return _bits(mask)
 
 
-def _helper(rank_core, topo):
+def _helpers(rank_core, topo):
     return [c for c in range(topo.CORES_PER_CHIP * topo.CHIPS)
-            if topo.chip(c) == topo.chip(rank_core) and topo.die(c) != topo.die(rank_core)][0]
+            if topo.chip(c) == topo.chip(rank_core) and topo.die(c) != topo.die(rank_core)][:2]
 
 
 def _masks(rank_core, T, topo):
     far = topo.mask(rank_core, [c for c in T.cores if c != rank_core][0])
-    return far, topo.mask(rank_core, _helper(rank_core, topo)) & ~far
+    return far, topo.mask(rank_core, _helpers(rank_core, topo)[0]) & ~far
 
 
 def rank_program(g, core, T, topo):
     S = T.sem
 
-    def codes(j, a=0, b=NC):
-        return lambda: T.xq[:, NC * j + a:NC * j + b].bitcast(dt.uint8)
+    def codes(j, hf):
+        return lambda: T.xq[:, NC * j + HF * hf:NC * j + HF * (hf + 1)].bitcast(dt.uint8)
 
     def plane(j):
         return lambda: T.xs[:, NC * j:NC * j + NC]
@@ -72,50 +73,59 @@ def rank_program(g, core, T, topo):
     r = T.rank_of(core)
     if r is None:
         for j, rc in enumerate(T.cores):
-            if core == _helper(rc, topo):
-                n = _bits(_masks(rc, T, topo)[1])
-                d = T.cores[(j + 4) % N]
-                m = topo.mask(core, d)
-                arr = S["xa%d" % j]
-                g.wait_ge(S.rc, n)
-                sent = _one(g, topo, d, codes(j, 0, HF), codes(j, 0, HF), m, arr, S.xl)
+            hs = _helpers(rc, topo)
+            if core not in hs:
+                continue
+            n = _bits(_masks(rc, T, topo)[1])
+            e3, e4 = T.cores[(j + 3) % N], T.cores[(j + 4) % N]
+            m = topo.mask(core, e4)
+            if core == hs[0]:
+                g.wait_ge(S.rca, n)
+                g.remote_dma_fused([_part(topo, [e4], codes(j, 0), m, S["xa%d" % j])], local_sem=S.xl)
                 g.wait_ge(S.rs, n)
-                sent += _one(g, topo, d, plane(j), plane(j), m, arr, S.xl)
-                sent += _one(g, topo, d, codes(j, HF, NC), codes(j, HF, NC), m, S.zb4, S.xl)
-                g.wait_ge(S.xl, sent)
+                g.remote_dma_fused([_part(topo, [e4], plane(j), m, S["xa%d" % j])], local_sem=S.xl)
+                g.wait_ge(S.xl, 2 * _bits(m))
+            else:
+                g.wait_ge(S.rcb, n)
+                g.remote_dma_fused([_part(topo, [e3, e4], codes(j, 1), m, S["xb%d" % j])], local_sem=S.xl)
+                g.wait_ge(S.xl, _bits(m))
         return
 
     v, s, t, q = g.vector, g.scalar, g.tensor, g.sync
-    own = slice(NC * r, NC * r + NC)
     d1, d2, d3 = [T.cores[(r + k) % N] for k in (1, 2, 3)]
     j1, j2, j3, j4 = [(r - k) % N for k in (1, 2, 3, 4)]
     Z = ((T.z0a, T.z1a), (T.z0b, T.z1b))
     Y = (T.ya, T.yb)
 
-    q.dma_start(T.xb[:], T.x[:]).then_inc(S.lx, 16)
+    q.dma_start(T.xb[:, 0:4 * HF], T.x[:, 0:4 * HF]).then_inc(S.lxa, 16)
+    s.dma_start(T.xb[:, 4 * HF:4 * NC], T.x[:, 4 * HF:4 * NC]).then_inc(S.lxb, 16)
     for p, (a, b) in enumerate(W1_PIECES):
         (s if p % 2 == 0 else q).dma_start(T.w1b[:, a:b], T.w1[:, a:b]).then_inc(S["lw%d" % p], 16)
     q.wait_ge(S["xa%d" % j2], 16)
     q.dma_start(T.w2b[:], T.w2[:]).then_inc(S.lv, 16)
 
-    v.wait_ge(S.lx, 16)
-    v.quantize_mx(T.xq[:, own], T.xs[:, own], T.xb[:]).then_inc(S.qx, 1)
+    o = NC * r
+    v.wait_ge(S.lxa, 16)
+    v.quantize_mx(T.xq[:, o:o + HF], T.xs[:, o:o + HF], T.xb[:, 0:4 * HF]).then_inc(S.qxa, 1)
+    v.wait_ge(S.lxb, 16)
+    v.quantize_mx(T.xq[:, o + HF:o + NC], T.xs[:, o + HF:o + NC], T.xb[:, 4 * HF:4 * NC]).then_inc(S.qxb, 1)
     for p, (a, b) in enumerate(W1_PIECES):
         v.wait_ge(S["lw%d" % p], 16)
         v.quantize_mx(T.w1q[:, a // 4:b // 4], T.w1s[:, a // 4:b // 4], T.w1b[:, a:b]).then_inc(S.qw, 1)
 
     far, near = _masks(core, T, topo)
-    hp = _helper(core, topo)
-    arr = S["xa%d" % r]
-    g.wait_ge(S.qx, 1)
-    g.remote_dma_fused([_part(topo, [hp], codes(r), codes(r), near, S.rc),
-                        _part(topo, [d1], codes(r), codes(r), far, arr)], local_sem=S.xl)
-    g.remote_dma_fused([_part(topo, [hp], plane(r), plane(r), near, S.rs),
-                        _part(topo, [d1, d2, d3], plane(r), plane(r), far, arr)], local_sem=S.xl)
-    sent = 2 * (_bits(near) + _bits(far))
-    sent += _one(g, topo, d2, codes(r), codes(r), far, arr, S.xl)
-    sent += _one(g, topo, d3, codes(r, 0, HF), codes(r, 0, HF), far, arr, S.xl)
-    sent += _one(g, topo, d3, codes(r, HF, NC), codes(r, HF, NC), far, S.zb3, S.xl)
+    ha, hb = _helpers(core, topo)
+    xa, xb = S["xa%d" % r], S["xb%d" % r]
+    g.wait_ge(S.qxa, 1)
+    g.remote_dma_fused([_part(topo, [ha], codes(r, 0), near, S.rca),
+                        _part(topo, [d1], codes(r, 0), far, xa)], local_sem=S.xl)
+    g.wait_ge(S.qxb, 1)
+    g.remote_dma_fused([_part(topo, [ha], plane(r), near, S.rs),
+                        _part(topo, [d1, d2, d3], plane(r), far, xa)], local_sem=S.xl)
+    g.remote_dma_fused([_part(topo, [hb], codes(r, 1), near, S.rcb),
+                        _part(topo, [d2, d3], codes(r, 0), far, xa)], local_sem=S.xl)
+    g.remote_dma_fused([_part(topo, [d1, d2], codes(r, 1), far, xb)], local_sem=S.xl)
+    sent = 3 * _bits(near) + 4 * _bits(far)
 
     def products(j, hf, first, last):
         c = NC * j + HF * hf
@@ -126,22 +136,17 @@ def rank_program(g, core, T, topo):
             if last:
                 mm.then_inc(S["zd%d%d" % (hf, i)], 1)
 
-    t.wait_ge(S.qx, 1)
+    t.wait_ge(S.qxa, 1)
+    t.wait_ge(S.qxb, 1)
     t.wait_ge(S.qw, len(W1_PIECES))
     products(r, 0, True, False)
     products(r, 1, True, False)
-    for j in (j1, j2):
+    for j in (j1, j2, j3, j4):
         t.wait_ge(S["xa%d" % j], 16)
-        products(j, 0, False, False)
-        products(j, 1, False, False)
-    t.wait_ge(S["xa%d" % j3], 16)
-    products(j3, 0, False, False)
-    t.wait_ge(S["xa%d" % j4], 16)
-    products(j4, 0, False, True)
-    t.wait_ge(S.zb3, 8)
-    products(j3, 1, False, False)
-    t.wait_ge(S.zb4, 8)
-    products(j4, 1, False, True)
+        products(j, 0, False, j == j4)
+    for j in (j1, j3, j2, j4):
+        t.wait_ge(S["xb%d" % j], 8)
+        products(j, 1, False, j == j4)
 
     prev = T.cores[(r - 1) % N]
     hmask = topo.mask(core, prev)

import numpy as np
from concourse.bass import DstId, RemoteDMATransfer
from concourse.mybir import dt, AluOpType, ActivationFunctionType

N = 5
NC = 256
HF = NC // 2
C = float(np.float32(0.0085))
W1_PIECES = [(0, 2048), (2048, 4096), (4096, 5120)]

SCRATCH = {
    "xb": ("sbuf", [128, 4 * NC], "bfloat16"),
    "w1b": ("sbuf", [128, 2 * N * 512], "bfloat16"),
    "w2b": ("sbuf", [128, 2 * 512], "bfloat16"),
    "hb": ("sbuf", [128, 4 * NC], "bfloat16"),
    "yo": ("sbuf", [128, NC], "float32"),
    "xq": ("sbuf", [128, N * NC], "float8_e4m3fn_x4"),
    "xs": ("sbuf", [128, N * NC], "uint8"),
    "w1q": ("sbuf", [128, 2 * N * 128], "float8_e4m3fn_x4"),
    "w1s": ("sbuf", [128, 2 * N * 128], "uint8"),
    "w2q": ("sbuf", [128, 2 * 128], "float8_e4m3fn_x4"),
    "w2s": ("sbuf", [128, 2 * 128], "uint8"),
    "hq": ("sbuf", [128, 2 * NC], "float8_e4m3fn_x4"),
    "hs": ("sbuf", [128, 2 * NC], "uint8"),
    "z0a": ("psum", [128, 512], "float32"),
    "z1a": ("psum", [128, 512], "float32"),
    "z0b": ("psum", [128, 512], "float32"),
    "z1b": ("psum", [128, 512], "float32"),
    "ya": ("psum", [128, 512], "float32"),
    "yb": ("psum", [128, 512], "float32"),
}
SEMAPHORES = ["lxa", "lxb", "lw0", "lw1", "lw2", "lv", "qxa", "qxb", "qw", "qv", "qh0", "qh1",
              "xa0", "xa1", "xa2", "xa3", "xa4", "xb0", "xb1", "xb2", "xb3", "xb4",
              "rca", "rcb", "rs", "xl", "zd00", "zd01", "zd10", "zd11", "hr0", "hr1", "ha0", "ha1", "hl0", "hl1",
              "yd0", "yd1", "yc0", "yc1", "sh0", "sh1", "sy0", "sy1"]


def _bits(mask):
    return bin(mask).count("1")


def _part(topo, dsts, ap, mask, remote_sem):
    return RemoteDMATransfer(dst_ids=[DstId(rid=topo.addr(d)[0], pnc=topo.addr(d)[1]) for d in dsts],
                             dma_engine_mask=mask, remote_sem=remote_sem, srcs=[ap()], dsts=[ap() for _ in dsts])


def _one(g, topo, d, src, dst, mask, remote_sem, local_sem):
    rid, pid, _ = topo.addr(d)
    g.remote_dma(out_ap=dst(), in_ap=src(), remote_sem=remote_sem, local_sem=local_sem,
                 pid=pid, routing_id=rid, dma_engine_mask=mask)
    return _bits(mask)


def _helpers(rank_core, topo):
    return [c for c in range(topo.CORES_PER_CHIP * topo.CHIPS)
            if topo.chip(c) == topo.chip(rank_core) and topo.die(c) != topo.die(rank_core)][:2]


def _masks(rank_core, T, topo):
    far = topo.mask(rank_core, [c for c in T.cores if c != rank_core][0])
    return far, topo.mask(rank_core, _helpers(rank_core, topo)[0]) & ~far


def rank_program(g, core, T, topo):
    S = T.sem

    def codes(j, hf):
        return lambda: T.xq[:, NC * j + HF * hf:NC * j + HF * (hf + 1)].bitcast(dt.uint8)

    def plane(j):
        return lambda: T.xs[:, NC * j:NC * j + NC]

    r = T.rank_of(core)
    if r is None:
        for j, rc in enumerate(T.cores):
            hs = _helpers(rc, topo)
            if core not in hs:
                continue
            n = _bits(_masks(rc, T, topo)[1])
            e3, e4 = T.cores[(j + 3) % N], T.cores[(j + 4) % N]
            m = topo.mask(core, e4)
            if core == hs[0]:
                g.wait_ge(S.rca, n)
                g.remote_dma_fused([_part(topo, [e4], codes(j, 0), m, S["xa%d" % j])], local_sem=S.xl)
                g.wait_ge(S.rs, n)
                g.remote_dma_fused([_part(topo, [e4], plane(j), m, S["xa%d" % j])], local_sem=S.xl)
                g.wait_ge(S.xl, 2 * _bits(m))
            else:
                g.wait_ge(S.rcb, n)
                g.remote_dma_fused([_part(topo, [e3, e4], codes(j, 1), m, S["xb%d" % j])], local_sem=S.xl)
                g.wait_ge(S.xl, _bits(m))
        return

    v, s, t, q = g.vector, g.scalar, g.tensor, g.sync
    d1, d2, d3 = [T.cores[(r + k) % N] for k in (1, 2, 3)]
    j1, j2, j3, j4 = [(r - k) % N for k in (1, 2, 3, 4)]
    Z = ((T.z0a, T.z1a), (T.z0b, T.z1b))
    Y = (T.ya, T.yb)

    q.dma_start(T.xb[:, 0:4 * HF], T.x[:, 0:4 * HF]).then_inc(S.lxa, 16)
    s.dma_start(T.xb[:, 4 * HF:4 * NC], T.x[:, 4 * HF:4 * NC]).then_inc(S.lxb, 16)
    for p, (a, b) in enumerate(W1_PIECES):
        (s if p % 2 == 0 else q).dma_start(T.w1b[:, a:b], T.w1[:, a:b]).then_inc(S["lw%d" % p], 16)
    q.wait_ge(S["xa%d" % j2], 16)
    q.dma_start(T.w2b[:], T.w2[:]).then_inc(S.lv, 16)

    o = NC * r
    v.wait_ge(S.lxa, 16)
    v.quantize_mx(T.xq[:, o:o + HF], T.xs[:, o:o + HF], T.xb[:, 0:4 * HF]).then_inc(S.qxa, 1)
    v.wait_ge(S.lxb, 16)
    v.quantize_mx(T.xq[:, o + HF:o + NC], T.xs[:, o + HF:o + NC], T.xb[:, 4 * HF:4 * NC]).then_inc(S.qxb, 1)
    for p, (a, b) in enumerate(W1_PIECES):
        v.wait_ge(S["lw%d" % p], 16)
        v.quantize_mx(T.w1q[:, a // 4:b // 4], T.w1s[:, a // 4:b // 4], T.w1b[:, a:b]).then_inc(S.qw, 1)

    far, near = _masks(core, T, topo)
    ha, hb = _helpers(core, topo)
    xa, xb = S["xa%d" % r], S["xb%d" % r]
    g.wait_ge(S.qxa, 1)
    g.remote_dma_fused([_part(topo, [ha], codes(r, 0), near, S.rca),
                        _part(topo, [d1], codes(r, 0), far, xa)], local_sem=S.xl)
    g.wait_ge(S.qxb, 1)
    g.remote_dma_fused([_part(topo, [ha], plane(r), near, S.rs),
                        _part(topo, [d1, d2, d3], plane(r), far, xa)], local_sem=S.xl)
    g.remote_dma_fused([_part(topo, [hb], codes(r, 1), near, S.rcb),
                        _part(topo, [d2, d3], codes(r, 0), far, xa)], local_sem=S.xl)
    g.remote_dma_fused([_part(topo, [d1, d2], codes(r, 1), far, xb)], local_sem=S.xl)
    sent = 3 * _bits(near) + 4 * _bits(far)

    def products(j, hf, first, last):
        c = NC * j + HF * hf
        for i in range(2):
            k = N * i + j
            mm = t.matmul_mx(Z[hf][i][:, 0:HF], T.w1q[:, 128 * k:128 * k + 128], T.w1s[:, 128 * k:128 * k + 128],
                             T.xq[:, c:c + HF], T.xs[:, c:c + HF], first, last)
            if last:
                mm.then_inc(S["zd%d%d" % (hf, i)], 1)

    t.wait_ge(S.qxa, 1)
    t.wait_ge(S.qxb, 1)
    t.wait_ge(S.qw, len(W1_PIECES))
    products(r, 0, True, False)
    products(r, 1, True, False)
    for j in (j1, j2, j3, j4):
        t.wait_ge(S["xa%d" % j], 16)
        products(j, 0, False, j == j4)
    for j in (j1, j3, j2, j4):
        t.wait_ge(S["xb%d" % j], 8)
        products(j, 1, False, j == j4)

    prev = T.cores[(r - 1) % N]
    hmask = topo.mask(core, prev)
    left = [0, 0]
    for hf in range(2):
        lo, hi = 4 * HF * hf, 4 * HF * (hf + 1)
        a, b = HF * hf, HF * (hf + 1)
        hr = S["hr%d" % hf]
        v.wait_ge(S["zd%d0" % hf], 1)
        v.tensor_scalar(T.hb[:, lo:hi:4], Z[hf][0][:, 0:HF], 0.0, C, AluOpType.max, AluOpType.mult).then_inc(hr, 1)
        v.tensor_scalar(T.hb[:, lo + 1:hi:4], Z[hf][0][:, 0:HF], -C, 0.0, AluOpType.mult, AluOpType.max).then_inc(hr, 1)
        s.wait_ge(S["zd%d1" % hf], 1)
        s.activation(T.hb[:, lo + 2:hi:4], Z[hf][1][:, 0:HF], ActivationFunctionType.Relu, scale=C).then_inc(hr, 1)
        s.activation(T.hb[:, lo + 3:hi:4], Z[hf][1][:, 0:HF], ActivationFunctionType.Relu, scale=-C).then_inc(hr, 1)
        v.wait_ge(hr, 4)
        v.quantize_mx(T.hq[:, a:b], T.hs[:, a:b], T.hb[:, lo:hi]).then_inc(S["qh%d" % hf], 1)
        g.wait_ge(S["qh%d" % hf], 1)
        left[hf] += _one(g, topo, prev, lambda: T.hq[:, a:b].bitcast(dt.uint8),
                         lambda: T.hq[:, NC + a:NC + b].bitcast(dt.uint8), hmask, S["ha%d" % hf], S["hl%d" % hf])
        left[hf] += _one(g, topo, prev, lambda: T.hs[:, a:b], lambda: T.hs[:, NC + a:NC + b], hmask,
                         S["ha%d" % hf], S["hl%d" % hf])

    for hf in range(2):
        lo, hi = 4 * HF * hf, 4 * HF * (hf + 1)
        s.wait_ge(S["hr%d" % hf], 4)
        s.wait_ge(S["hl%d" % hf], left[hf])
        s.dma_start(T.h[:, lo:hi], T.hb[:, lo:hi]).then_inc(S["sh%d" % hf], 16)

    v.wait_ge(S.lv, 16)
    v.quantize_mx(T.w2q[:], T.w2s[:], T.w2b[:]).then_inc(S.qv, 1)
    t.wait_ge(S.qv, 1)
    for hf in range(2):
        a, b = HF * hf, HF * (hf + 1)
        t.wait_ge(S["qh%d" % hf], 1)
        t.matmul_mx(Y[hf][:, 0:HF], T.w2q[:, 0:128], T.w2s[:, 0:128], T.hq[:, a:b], T.hs[:, a:b], True, False)
    for hf in range(2):
        a, b = HF * hf, HF * (hf + 1)
        t.wait_ge(S["ha%d" % hf], 16)
        t.matmul_mx(Y[hf][:, 0:HF], T.w2q[:, 128:256], T.w2s[:, 128:256], T.hq[:, NC + a:NC + b],
                    T.hs[:, NC + a:NC + b], False, True).then_inc(S["yd%d" % hf], 1)
        v.wait_ge(S["yd%d" % hf], 1)
        v.tensor_copy(T.yo[:, a:b], Y[hf][:, 0:HF]).then_inc(S["yc%d" % hf], 1)
        q.wait_ge(S["yc%d" % hf], 1)
        q.dma_start(T.y[:, a:b], T.yo[:, a:b]).then_inc(S["sy%d" % hf], 16)

    g.wait_ge(S.xl, sent)
    for hf in range(2):
        s.wait_ge(S["sh%d" % hf], 16)
        q.wait_ge(S["sy%d" % hf], 16)
